import numpy as np
import ml_dtypes


def mxq(x, axis, fmt="e4m3"):
    dtype, down = {"e4m3": (ml_dtypes.float8_e4m3fn, 7), "e5m2": (ml_dtypes.float8_e5m2, 14)}[fmt]
    v = np.moveaxis(np.asarray(x, np.float32).astype(ml_dtypes.bfloat16).astype(np.float64), axis, -1)
    blocks = v.reshape(v.shape[:-1] + (-1, 32))
    amax = np.abs(blocks).max(-1, keepdims=True)
    byte = np.maximum(np.where(amax > 0, np.frexp(amax)[1] - 1 + 127, 0) - down, 1)
    scale = np.exp2(byte - 127.0)
    codes = (blocks / scale).astype(np.float32).astype(dtype).astype(np.float64)
    return np.moveaxis((codes * scale).reshape(v.shape), -1, axis)


WIDE = False


def mx_kscale(k):
    if not WIDE:
        return np.ones(k)
    levels = np.array([10, -10, 5, -5, 0])
    if k % 512:
        return np.exp2(np.random.permutation(np.resize(levels, k // 32))).repeat(32)
    a = np.empty((k // 512, 16))
    for p in range(k // 512):
        a[p, :8] = np.random.permutation(np.resize(levels, 8))
        for g in range(8):
            far = levels[np.abs(levels - a[p, g]) >= 10]
            a[p, g + 8] = far[np.random.randint(len(far))]
    return np.exp2(a.ravel()).repeat(32)


BF16 = ml_dtypes.bfloat16


def bf(x):
    return np.asarray(x, np.float32).astype(BF16)


def f64(x):
    return np.asarray(x).astype(np.float64)


E2M1 = np.array([0.0, 0.5, 1.0, 1.5, 2.0, 3.0, 4.0, 6.0, -0.0, -0.5, -1.0, -1.5, -2.0, -3.0, -4.0, -6.0])


def pack_weight(w, fmt):
    k, n = w.shape
    w = f64(bf(w)).reshape(k // 32, 32, n)
    amax = np.abs(w).max(1)
    if fmt == "e4m3":
        byte = np.frexp(amax)[1] - 1 + 127 - 7
    else:
        mant, ex = np.frexp(amax / 6.0)
        byte = np.where(mant > 0.5, ex, ex - 1) + 127
    byte = np.clip(np.where(amax > 0, byte, 1), 1, 254)
    scaled = (w * np.exp2(127.0 - byte)[:, None, :]).reshape(k, n).astype(np.float32)
    by_word = np.ascontiguousarray(scaled.reshape(k // 512, 128, 4, n).transpose(0, 1, 3, 2))
    if fmt == "e4m3":
        words = by_word.astype(ml_dtypes.float8_e4m3fn).view(np.uint8)
    else:
        c = by_word.astype(ml_dtypes.float4_e2m1fn).view(np.uint8) & 0xF
        words = c[..., 0::2] | (c[..., 1::2] << 4)
    return np.ascontiguousarray(words), np.ascontiguousarray(byte.astype(np.uint8).reshape(k // 512, 16, n))


def unpack_weight(words, scales, fmt):
    g, p, n, _ = words.shape
    if fmt == "e4m3":
        vals = np.ascontiguousarray(words).view(ml_dtypes.float8_e4m3fn).astype(np.float64)
    else:
        nib = np.empty((g, p, n, 4), np.uint8)
        nib[..., 0::2] = words & 0xF
        nib[..., 1::2] = words >> 4
        vals = E2M1[nib]
    vals = vals * np.repeat(np.exp2(scales.astype(np.float64) - 127.0), 8, axis=1)[..., None]
    return vals.transpose(0, 1, 3, 2).reshape(g * 512, n)
def pack4(w):
    words, scales = pack_weight(w, "e2m1")
    return words.reshape(words.shape[0], 128, -1), scales


def unpack4(words, scales):
    return unpack_weight(words.reshape(words.shape[0], 128, -1, 2), scales, "e2m1")


def planes(Y):
    n, m = Y.shape
    b = f64(bf(Y)).reshape(n // 32, 32, m)
    amax = np.abs(b).max(1)
    byte = np.clip(np.where(amax > 0, np.frexp(amax)[1] - 1 + 127 - 7, 1), 1, 254)
    codes = (b * np.exp2(127.0 - byte)[:, None, :]).reshape(n, m).astype(np.float32).astype(ml_dtypes.float8_e4m3fn).view(np.uint8)
    words = codes.reshape(n // 512, 128, 4, m).transpose(0, 1, 3, 2)
    return np.ascontiguousarray(words), np.ascontiguousarray(byte.astype(np.uint8).reshape(n // 512, 16, m))


N, D, K = 1024, 512, 2048

STUDENT_TEMP = 0.1
TEACHER_TEMP = 0.07


def softmax(v):
    e = np.exp(v - v.max(-1, keepdims=True))
    return e / e.sum(-1, keepdims=True)


def setup_inputs():
    s = mx_kscale(D)
    u = mx_kscale(D)
    t = mx_kscale(K)
    hs = bf(np.random.standard_normal((N, D)) * STUDENT_TEMP / np.sqrt(D))
    c = bf((1.0 + 0.1 * np.random.standard_normal(D)) * s)
    vs = bf(np.random.standard_normal((D, K)) / s[:, None] / t[None, :])
    gs = bf((1.0 + 0.1 * np.random.standard_normal(K)) * t)
    ht = bf(np.random.standard_normal((N, D)) * TEACHER_TEMP * u)
    vt_words, vt_scales = pack4(np.random.standard_normal((D, K)) / np.sqrt(D) / u[:, None])
    ctr = bf(np.random.standard_normal(K) * 0.05)
    return {
        "hs": hs,
        "c": c,
        "vs": vs,
        "gs": gs,
        "ht": ht,
        "vt_words": vt_words,
        "vt_scales": vt_scales,
        "ctr": ctr,
    }


def student_logits(hs, c, vs, gs):
    scaled = hs * c[None, :]
    return gs[None, :] * (mxq(scaled, 1, "e4m3") @ mxq(vs, 0, "e4m3"))


def teacher_probs(ht, vt_words, vt_scales, ctr):
    zt = mxq(ht, 1, "e4m3") @ unpack4(vt_words, vt_scales)
    return softmax((zt - ctr[None, :]) / TEACHER_TEMP)


def core(hs, c, vs, gs, ht, vt_words, vt_scales, ctr):
    hs, c, vs, gs, ht, ctr = f64(hs), f64(c), f64(vs), f64(gs), f64(ht), f64(ctr)
    zs = student_logits(hs, c, vs, gs)
    pt = teacher_probs(ht, vt_words, vt_scales, ctr)
    ps = softmax(zs / STUDENT_TEMP)
    g = gs[None, :] * (ps - pt) / STUDENT_TEMP
    return c[None, :] * (mxq(g, 1, "e4m3") @ mxq(vs, 1, "e4m3").T)


def reference(hs, c, vs, gs, ht, vt_words, vt_scales, ctr):
    R_out = core(hs, c, vs, gs, ht, vt_words, vt_scales, ctr)
    words, scales = planes(R_out.T)
    return R_out, words, scales

from contextlib import ExitStack

import concourse.mybir as mybir
from concourse.masks import make_identity

N, D, K = 1024, 512, 2048
STUDENT_TEMP = 0.1
TEACHER_TEMP = 0.07
FLOPS = 3 * 2 * N * D * K

F32 = mybir.dt.float32
BF16 = mybir.dt.bfloat16
U32 = mybir.dt.uint32
I32 = mybir.dt.int32
U8 = mybir.dt.uint8
FP8X4 = mybir.dt.float8_e4m3fn_x4
FP4X4 = mybir.dt.float4_e2m1fn_x4
ALU = mybir.AluOpType
ACT = mybir.ActivationFunctionType

P = 128
PACK = 4
BANK = 512
TILES = N // P
PAIRS = TILES // 2
GROUPS = K // BANK
C_ROW = 4
GS_ROW = 32


PARAMS = {"rings": {"vector": 4, "scalar": 4}}
STREAMS = {'clear': [('clear', ())], 'load_vs': [('load_vs', (0,)), ('load_vs', (1,)), ('load_vs', (2,)), ('load_vs', (3,))], 'load_ctr_rows': [('load_ctr_rows', ())], 'load_tokens_ht': [('load_tokens', ('ht', 0)), ('load_tokens', ('ht', 1)), ('load_tokens', ('ht', 2)), ('load_tokens', ('ht', 3))], 'spread_row': [('spread_row', (0,)), ('spread_row', (1,)), ('spread_row', (2,)), ('spread_row', (3,)), ('spread_row', (4,))], 'load_vt_scales': [('load_vt_scales', ())], 'group_vs': [('group_vs', (0, 'gpsimd')), ('group_vs', (1, 'gpsimd')), ('group_vs', (2, 'gpsimd')), ('group_vs', (3, 'gpsimd'))], 'turn_tokens_ht': [('turn_tokens', ('ht', 0)), ('turn_tokens', ('ht', 1)), ('turn_tokens', ('ht', 2)), ('turn_tokens', ('ht', 3))], 'load_vt': [('load_vt', (0,)), ('load_vt', (1,))], 'quantise_tokens_ht': [('quantise_tokens', ('ht', 0)), ('quantise_tokens', ('ht', 1)), ('quantise_tokens', ('ht', 2)), ('quantise_tokens', ('ht', 3))], 'turn_vs': [('turn_vs', (0, 0)), ('turn_vs', (0, 1)), ('turn_vs', (1, 0)), ('turn_vs', (1, 1)), ('turn_vs', (2, 0)), ('turn_vs', (2, 1)), ('turn_vs', (3, 0)), ('turn_vs', (3, 1))], 'quantise_vs': [('quantise_vs', (0,)), ('quantise_vs', (1,)), ('quantise_vs', (2,)), ('quantise_vs', (3,))], 'load_c_row': [('load_c_row', ())], 'teacher_logits': [('teacher_logits', (0, 0)), ('teacher_logits', (0, 1)), ('teacher_logits', (0, 2)), ('teacher_logits', (0, 3)), ('teacher_logits', (1, 0)), ('teacher_logits', (1, 1)), ('teacher_logits', (1, 2)), ('teacher_logits', (1, 3)), ('teacher_logits', (2, 0)), ('teacher_logits', (2, 1)), ('teacher_logits', (2, 2)), ('teacher_logits', (2, 3)), ('teacher_logits', (3, 0)), ('teacher_logits', (3, 1)), ('teacher_logits', (3, 2)), ('teacher_logits', (3, 3)), ('teacher_logits', (4, 0)), ('teacher_logits', (4, 1)), ('teacher_logits', (4, 2)), ('teacher_logits', (4, 3)), ('teacher_logits', (5, 0)), ('teacher_logits', (5, 1)), ('teacher_logits', (5, 2)), ('teacher_logits', (5, 3)), ('teacher_logits', (6, 0)), ('teacher_logits', (6, 1)), ('teacher_logits', (6, 2)), ('teacher_logits', (6, 3)), ('teacher_logits', (7, 0)), ('teacher_logits', (7, 1)), ('teacher_logits', (7, 2)), ('teacher_logits', (7, 3))], 'load_gs_rows': [('load_gs_rows', ())], 'load_tokens_hs': [('load_tokens', ('hs', 0)), ('load_tokens', ('hs', 1)), ('load_tokens', ('hs', 2)), ('load_tokens', ('hs', 3))], 'scale_hs': [('scale_hs', (0, 'vector')), ('scale_hs', (1, 'vector')), ('scale_hs', (2, 'vector')), ('scale_hs', (3, 'vector'))], 'gs_columns': [('gs_columns', ())], 'turn_tokens_hs': [('turn_tokens', ('hs', 0)), ('turn_tokens', ('hs', 1)), ('turn_tokens', ('hs', 2)), ('turn_tokens', ('hs', 3))], 'teacher_fold': [('teacher_fold', (0,)), ('teacher_fold', (1,)), ('teacher_fold', (2,)), ('teacher_fold', (3,)), ('teacher_fold', (4,)), ('teacher_fold', (5,)), ('teacher_fold', (6,)), ('teacher_fold', (7,))], 'quantise_tokens_hs': [('quantise_tokens', ('hs', 0)), ('quantise_tokens', ('hs', 1)), ('quantise_tokens', ('hs', 2)), ('quantise_tokens', ('hs', 3))], 'teacher_min': [('teacher_min', (0,)), ('teacher_min', (1,)), ('teacher_min', (2,)), ('teacher_min', (3,)), ('teacher_min', (4,)), ('teacher_min', (5,)), ('teacher_min', (6,)), ('teacher_min', (7,))], 'student_logits': [('student_logits', (0, 0)), ('student_logits', (0, 1)), ('student_logits', (0, 2)), ('student_logits', (0, 3)), ('student_logits', (0, 4)), ('student_logits', (0, 5)), ('student_logits', (0, 6)), ('student_logits', (0, 7)), ('student_logits', (1, 0)), ('student_logits', (1, 1)), ('student_logits', (1, 2)), ('student_logits', (1, 3)), ('student_logits', (1, 4)), ('student_logits', (1, 5)), ('student_logits', (1, 6)), ('student_logits', (1, 7)), ('student_logits', (2, 0)), ('student_logits', (2, 1)), ('student_logits', (2, 2)), ('student_logits', (2, 3)), ('student_logits', (2, 4)), ('student_logits', (2, 5)), ('student_logits', (2, 6)), ('student_logits', (2, 7)), ('student_logits', (3, 0)), ('student_logits', (3, 1)), ('student_logits', (3, 2)), ('student_logits', (3, 3)), ('student_logits', (3, 4)), ('student_logits', (3, 5)), ('student_logits', (3, 6)), ('student_logits', (3, 7))], 'quantise_vsT': [('quantise_vsT', (0,)), ('quantise_vsT', (1,)), ('quantise_vsT', (2,)), ('quantise_vsT', (3,))], 'load_columns': [('load_columns', ())], 'scale_columns': [('scale_columns', ())], 'student_turn': [('student_turn', (0, 0)), ('student_turn', (0, 1)), ('student_turn', (0, 2)), ('student_turn', (0, 3)), ('student_turn', (1, 0)), ('student_turn', (1, 1)), ('student_turn', (1, 2)), ('student_turn', (1, 3)), ('student_turn', (2, 0)), ('student_turn', (2, 1)), ('student_turn', (2, 2)), ('student_turn', (2, 3)), ('student_turn', (3, 0)), ('student_turn', (3, 1)), ('student_turn', (3, 2)), ('student_turn', (3, 3)), ('student_turn', (4, 0)), ('student_turn', (4, 1)), ('student_turn', (4, 2)), ('student_turn', (4, 3)), ('student_turn', (5, 0)), ('student_turn', (5, 1)), ('student_turn', (5, 2)), ('student_turn', (5, 3)), ('student_turn', (6, 0)), ('student_turn', (6, 1)), ('student_turn', (6, 2)), ('student_turn', (6, 3)), ('student_turn', (7, 0)), ('student_turn', (7, 1)), ('student_turn', (7, 2)), ('student_turn', (7, 3))], 'softmax_exp_teacher': [('softmax_exp', ('teacher', 0)), ('softmax_exp', ('teacher', 1)), ('softmax_exp', ('teacher', 2)), ('softmax_exp', ('teacher', 3)), ('softmax_exp', ('teacher', 4)), ('softmax_exp', ('teacher', 5)), ('softmax_exp', ('teacher', 6)), ('softmax_exp', ('teacher', 7))], 'invert_total_teacher': [('invert_total', ('teacher', 0)), ('invert_total', ('teacher', 1)), ('invert_total', ('teacher', 2)), ('invert_total', ('teacher', 3)), ('invert_total', ('teacher', 4)), ('invert_total', ('teacher', 5)), ('invert_total', ('teacher', 6)), ('invert_total', ('teacher', 7))], 'softmax_exp_student': [('softmax_exp', ('student', 0)), ('softmax_exp', ('student', 1)), ('softmax_exp', ('student', 2)), ('softmax_exp', ('student', 3)), ('softmax_exp', ('student', 4)), ('softmax_exp', ('student', 5)), ('softmax_exp', ('student', 6)), ('softmax_exp', ('student', 7))], 'invert_total_student': [('invert_total', ('student', 0)), ('invert_total', ('student', 1)), ('invert_total', ('student', 2)), ('invert_total', ('student', 3)), ('invert_total', ('student', 4)), ('invert_total', ('student', 5)), ('invert_total', ('student', 6)), ('invert_total', ('student', 7))], 'normalise_teacher': [('normalise', ('teacher', 0, 0, 2, 'gpsimd')), ('normalise', ('teacher', 0, 1, 2, 'gpsimd')), ('normalise', ('teacher', 1, 0, 2, 'gpsimd')), ('normalise', ('teacher', 1, 1, 2, 'gpsimd')), ('normalise', ('teacher', 2, 0, 2, 'gpsimd')), ('normalise', ('teacher', 2, 1, 2, 'gpsimd')), ('normalise', ('teacher', 3, 0, 2, 'gpsimd')), ('normalise', ('teacher', 3, 1, 2, 'gpsimd')), ('normalise', ('teacher', 4, 0, 2, 'gpsimd')), ('normalise', ('teacher', 4, 1, 2, 'gpsimd')), ('normalise', ('teacher', 5, 0, 2, 'gpsimd')), ('normalise', ('teacher', 5, 1, 2, 'gpsimd')), ('normalise', ('teacher', 6, 0, 2, 'gpsimd')), ('normalise', ('teacher', 6, 1, 2, 'gpsimd')), ('normalise', ('teacher', 7, 0, 2, 'gpsimd')), ('normalise', ('teacher', 7, 1, 2, 'gpsimd'))], 'normalise_student': [('normalise', ('student', 0, 0, 2, 'gpsimd')), ('normalise', ('student', 0, 1, 2, 'gpsimd')), ('normalise', ('student', 1, 0, 2, 'gpsimd')), ('normalise', ('student', 1, 1, 2, 'gpsimd')), ('normalise', ('student', 2, 0, 2, 'gpsimd')), ('normalise', ('student', 2, 1, 2, 'gpsimd')), ('normalise', ('student', 3, 0, 2, 'gpsimd')), ('normalise', ('student', 3, 1, 2, 'gpsimd')), ('normalise', ('student', 4, 0, 2, 'gpsimd')), ('normalise', ('student', 4, 1, 2, 'gpsimd')), ('normalise', ('student', 5, 0, 2, 'gpsimd')), ('normalise', ('student', 5, 1, 2, 'gpsimd')), ('normalise', ('student', 6, 0, 2, 'gpsimd')), ('normalise', ('student', 6, 1, 2, 'gpsimd')), ('normalise', ('student', 7, 0, 4, 'vector')), ('normalise', ('student', 7, 1, 4, 'vector')), ('normalise', ('student', 7, 2, 4, 'vector')), ('normalise', ('student', 7, 3, 4, 'vector'))], 'grad_turn': [('grad_turn', (0, 0)), ('grad_turn', (0, 1)), ('grad_turn', (0, 2)), ('grad_turn', (0, 3)), ('grad_turn', (1, 0)), ('grad_turn', (1, 1)), ('grad_turn', (1, 2)), ('grad_turn', (1, 3)), ('grad_turn', (2, 0)), ('grad_turn', (2, 1)), ('grad_turn', (2, 2)), ('grad_turn', (2, 3)), ('grad_turn', (3, 0)), ('grad_turn', (3, 1)), ('grad_turn', (3, 2)), ('grad_turn', (3, 3)), ('grad_turn', (4, 0)), ('grad_turn', (4, 1)), ('grad_turn', (4, 2)), ('grad_turn', (4, 3)), ('grad_turn', (5, 0)), ('grad_turn', (5, 1)), ('grad_turn', (5, 2)), ('grad_turn', (5, 3)), ('grad_turn', (6, 0)), ('grad_turn', (6, 1)), ('grad_turn', (6, 2)), ('grad_turn', (6, 3)), ('grad_turn', (7, 0)), ('grad_turn', (7, 1)), ('grad_turn', (7, 2)), ('grad_turn', (7, 3))], 'quantise_grad': [('quantise_grad', (0, 0, 4)), ('quantise_grad', (1, 0, 4)), ('quantise_grad', (2, 0, 4)), ('quantise_grad', (3, 0, 4)), ('quantise_grad', (4, 0, 4)), ('quantise_grad', (5, 0, 4)), ('quantise_grad', (6, 0, 4)), ('quantise_grad', (7, 0, 1)), ('quantise_grad', (7, 1, 1)), ('quantise_grad', (7, 2, 1)), ('quantise_grad', (7, 3, 1))], 'feature_grad': [('feature_grad', (0,)), ('feature_grad', (1,)), ('feature_grad', (2,)), ('feature_grad', (3,)), ('feature_grad', (4,)), ('feature_grad', (5,)), ('feature_grad', (6,))], 'group_result': [('group_result', (0, 'scalar')), ('group_result', (1, 'scalar')), ('group_result', (2, 'scalar')), ('group_result', (3, 'scalar')), ('group_result', (4, 'scalar')), ('group_result', (5, 'scalar')), ('group_result', (6, 'scalar')), ('group_result', (7, 'vector'))], 'store_result': [('store_result', (0,)), ('store_result', (1,)), ('store_result', (2,)), ('store_result', (3,)), ('store_result', (4,)), ('store_result', (5,)), ('store_result', (6,)), ('store_result', (7,))], 'store_codes': [('store_codes', (0,)), ('store_codes', (1,)), ('store_codes', (2,)), ('store_codes', (3,)), ('store_codes', (4,)), ('store_codes', (5,)), ('store_codes', (6,)), ('store_codes', (7,))], 'store_scales': [('store_scales', (0, 7)), ('store_scales', (7, 8))], 'last_feature_passes': [('last_feature_passes', (0,)), ('last_feature_passes', (1,)), ('last_feature_passes', (2,)), ('last_feature_passes', (3,))], 'last_feature_grad': [('last_feature_grad', ())], 'warm_exp': [('warm_exp', ())]}
WEAVE = """
clear load_vs load_ctr_rows load_tokens_ht spread_row load_vt_scales group_vs turn_tokens_ht load_vt
quantise_tokens_ht load_vs load_vt turn_vs spread_row quantise_vs load_c_row spread_row teacher_logits*2
spread_row group_vs load_tokens_ht teacher_logits load_gs_rows teacher_logits*2 load_tokens_hs spread_row
turn_tokens_ht turn_vs scale_hs quantise_vs load_tokens_hs gs_columns scale_hs turn_tokens_hs load_vs
teacher_fold quantise_tokens_ht quantise_tokens_hs turn_vs load_tokens_hs teacher_min turn_tokens_hs
teacher_logits*2 student_logits*2 group_vs teacher_logits*2 load_vs quantise_vsT quantise_vs scale_hs
load_columns student_logits group_vs scale_columns student_turn turn_vs teacher_logits student_logits*2
teacher_logits student_logits teacher_logits student_turn teacher_logits softmax_exp_teacher teacher_logits
quantise_vs load_tokens_ht*2 turn_vs turn_tokens_hs quantise_tokens_hs teacher_fold turn_tokens_ht
teacher_logits student_logits load_tokens_hs student_logits quantise_tokens_hs student_logits
invert_total_teacher quantise_tokens_ht scale_hs teacher_min student_logits teacher_logits student_turn
student_logits teacher_logits student_logits turn_tokens_hs student_turn teacher_logits student_logits
softmax_exp_student student_turn student_logits turn_tokens_ht teacher_fold softmax_exp_teacher quantise_vsT
invert_total_student teacher_fold student_turn teacher_logits student_turn normalise_teacher*2 student_logits
teacher_logits teacher_min normalise_student turn_vs invert_total_teacher student_logits student_turn
softmax_exp_student teacher_logits grad_turn*2 teacher_min turn_vs normalise_student student_turn grad_turn
normalise_teacher quantise_tokens_hs invert_total_student quantise_vsT student_turn softmax_exp_teacher
turn_vs student_logits*3 teacher_logits*2 student_turn normalise_teacher teacher_logits student_turn grad_turn
invert_total_teacher quantise_tokens_ht student_logits quantise_vsT quantise_grad normalise_student
student_logits*2 teacher_fold*2 student_logits softmax_exp_student student_turn grad_turn student_turn
normalise_student softmax_exp_teacher teacher_logits student_logits feature_grad normalise_teacher
student_logits normalise_teacher student_logits student_turn invert_total_student invert_total_teacher
grad_turn*2 group_result normalise_student grad_turn normalise_student student_turn teacher_min
softmax_exp_student student_turn normalise_teacher store_result normalise_teacher student_logits*2
teacher_logits*2 grad_turn softmax_exp_teacher grad_turn student_turn invert_total_student store_codes
normalise_student quantise_grad student_turn grad_turn student_turn teacher_min grad_turn softmax_exp_student
normalise_student student_logits invert_total_teacher softmax_exp_teacher student_logits feature_grad
teacher_logits normalise_teacher student_turn group_result grad_turn invert_total_student quantise_grad
teacher_fold grad_turn student_turn grad_turn student_turn student_logits feature_grad normalise_student
invert_total_teacher normalise_student teacher_logits student_logits normalise_teacher teacher_logits
teacher_min student_turn grad_turn student_turn grad_turn normalise_teacher softmax_exp_student
softmax_exp_teacher grad_turn*2 student_turn invert_total_student normalise_teacher quantise_grad
normalise_student store_codes store_result grad_turn normalise_student group_result student_turn
teacher_logits*2 feature_grad student_turn invert_total_teacher store_result normalise_teacher quantise_grad
softmax_exp_student store_codes group_result teacher_fold student_turn invert_total_student grad_turn
normalise_student student_turn teacher_min student_turn feature_grad normalise_student grad_turn*2
normalise_teacher grad_turn group_result softmax_exp_teacher student_turn store_result grad_turn*2
softmax_exp_student invert_total_teacher quantise_grad store_codes store_result grad_turn invert_total_student
grad_turn normalise_student quantise_grad normalise_teacher store_codes normalise_teacher feature_grad
normalise_student*2 group_result grad_turn normalise_student store_codes feature_grad quantise_grad grad_turn
quantise_grad group_result store_result store_codes grad_turn*2 store_scales store_result last_feature_passes
quantise_grad last_feature_passes*2 quantise_grad last_feature_passes last_feature_grad group_result
store_codes store_result store_scales warm_exp
"""


def make_plan(q):
    taken = {}
    plan = []
    for word in WEAVE.split():
        kind, count = (word + "*1").split("*")[:2]
        for n in range(int(count)):
            plan.append(STREAMS[kind][taken.get(kind, 0)])
            taken[kind] = taken.get(kind, 0) + 1
    return plan


def tile_dinocentredstudentfeaturegrad_x2_kernel(tc, hs, c, vs, gs, ht, vt_words, vt_scales, ctr, out_0, out_1, out_2):
    nc = tc.nc
    with ExitStack() as ctx:
        keep = ctx.enter_context(tc.tile_pool(name="keep", bufs=1))
        work = ctx.enter_context(tc.tile_pool(name="work", bufs=2))
        psum = ctx.enter_context(tc.psum_pool(name="psum", bufs=1))

        def new_bank(reader):
            return psum.tile([P, BANK], F32, name=reader + "_bank", bufs=PARAMS["rings"][reader])

        def kept(name, shape, dtype):
            return keep.tile(shape, dtype, name=name, align_bytes=64)

        def passing(name, shape, dtype, bufs):
            return work.tile(shape, dtype, name=name, bufs=bufs, align_bytes=64)

        ident32 = kept("ident32", [P, P], F32)
        ident16 = kept("ident16", [P, P], BF16)
        rows = kept("rows", [P, BANK], BF16)
        rows1 = kept("rows1", [P, BANK], BF16)
        rows2 = kept("rows2", [P, P], BF16)
        warm = kept("warm", [P, 2], F32)
        ctr_all = kept("ctr_all", [P, GROUPS, BANK], BF16)
        c_all = kept("c_all", [P, D], BF16)
        gs_logit = kept("gs_logit", [P, K // P], F32)
        gs_raw = kept("gs_raw", [P, GROUPS, PACK], BF16)
        gs_grad = kept("gs_grad", [P, GROUPS, PACK], F32)
        c_raw = kept("c_raw", [P, PACK], BF16)
        c_out = kept("c_out", [P, PACK], F32)
        vt_codes = kept("vt_codes", [P, 2 * K], U8)
        vt_plane = kept("vt_plane", [P, K], U8)
        out_codes = kept("out_codes", [P, N], U32)
        out_plane = kept("out_plane", [P, N], U8)
        vs_raw = [kept("vs_raw%d" % g, [P, PACK, BANK], BF16) for g in range(GROUPS)]
        raw = {}
        for which in ("ht", "hs"):
            for j in range(PAIRS):
                raw[which, j] = kept("%s_raw%d" % (which, j), [P, 2, D], BF16)

        live = {}

        def quantise(name, width, keep_as, bufs):
            src = live[name]
            codes = passing(keep_as[0] + "_codes", [P, width // PACK], U32, bufs)
            plane = passing(keep_as[0] + "_plane", [P, width // PACK], U8, bufs)
            nc.vector.quantize_mx(out=codes[:].bitcast(FP8X4), scales=plane[:], in_=src[:])
            live[keep_as] = (codes, plane)

        def load_tokens(which, j):
            src = ht if which == "ht" else hs
            nc.sync.dma_start(out=raw[which, j][:], in_=src[2 * P * j : 2 * P * (j + 1), :].rearrange("(i p) d -> p i d", p=P))

        def load_vs(g):
            nc.sync.dma_start(out=vs_raw[g][:], in_=vs[:, g * BANK : (g + 1) * BANK].rearrange("(p j) k -> p j k", j=PACK))

        def load_vt(h):
            half = slice(h * K // 4, (h + 1) * K // 4)
            nc.sync.dma_start(out=vt_codes[:].bitcast(I32)[:, half], in_=vt_words[0].bitcast(I32)[:, half])

        def load_vt_scales():
            for q in range(4):
                nc.sync.dma_start(out=vt_plane[32 * q : 32 * q + 4, :].bitcast(I32), in_=vt_scales[0, 4 * q : 4 * q + 4, :].bitcast(I32))

        def load_ctr_rows():
            nc.scalar.dma_start(out=rows[0:GROUPS, :], in_=ctr.rearrange("(g n) -> g n", n=BANK))

        def load_c_row():
            nc.sync.dma_start(out=rows1[0:1, :], in_=c.rearrange("(g n) -> g n", n=D))

        def load_gs_rows():
            nc.sync.dma_start(out=rows2[0 : K // P, :], in_=gs.rearrange("(g n) -> g n", n=P))

        def load_columns():
            nc.sync.dma_start(out=gs_raw[:], in_=gs.rearrange("(g p t) -> p g t", p=P, t=PACK))
            nc.sync.dma_start(out=c_raw[:], in_=c.rearrange("(p t) -> p t", t=PACK))

        def clear():
            nc.vector.memset(rows[:].bitcast(U32), 0)
            nc.vector.memset(vt_plane[:].bitcast(U32), 0)
            nc.vector.memset(warm[:, 0:1], 0.0)
            nc.vector.memset(rows1[:].bitcast(U32), 0)
            nc.vector.memset(rows2[:].bitcast(U32), 0)
            make_identity(nc, ident16[:])
            make_identity(nc, ident32[:])

        def warm_exp():
            nc.scalar.activation(out=warm[:, 1:2], in_=warm[:, 0:1], func=ACT.Exp)

        def spread_row(r):
            bank = new_bank("scalar")
            src, row = (rows1, 0) if r == C_ROW else (rows, r)
            nc.tensor.matmul(bank[:], lhsT=ident16[:, row : row + 1].to_broadcast([P, P]), rhs=src[:], start=True, stop=True)
            if r == C_ROW:
                nc.scalar.copy(out=c_all[:], in_=bank[:])
            else:
                nc.scalar.copy(out=ctr_all[:, r, :].rearrange("p (t m) -> p t m", t=PACK), in_=bank[:].rearrange("p (m t) -> p t m", t=PACK))

        def gs_columns():
            bank = new_bank("scalar")
            nc.tensor.matmul(bank[:, 0:P], lhsT=rows2[:], rhs=ident16[:], start=True, stop=True)
            nc.scalar.activation(out=gs_logit[:], in_=bank[:, 0 : K // P], func=ACT.Copy, scale=-1.0 / STUDENT_TEMP)

        def scale_columns():
            nc.scalar.activation(out=gs_grad[:], in_=gs_raw[:], func=ACT.Copy, scale=1.0 / STUDENT_TEMP)
            nc.scalar.copy(out=c_out[:], in_=c_raw[:])

        def scale_hs(j, engine):
            scaled = passing("scaled", [P, 2, D], BF16, 2)
            for i in range(2):
                (nc.vector if engine == "vector" else nc.gpsimd).tensor_tensor(out=scaled[:, i, :], in0=raw["hs", j][:, i, :], in1=c_all[:], op=ALU.mult)
            live["scaled", j] = scaled

        def turn_tokens(which, j):
            src = raw["ht", j] if which == "ht" else live["scaled", j]
            bank = new_bank("scalar")
            turned = bank[:].rearrange("p (i u n) -> p i u n", i=2, u=2)
            for i in range(2):
                words = src[:, i, :].bitcast(F32)
                for u in range(2):
                    nc.tensor.transpose(turned[:, i, u, :], words[:, u::2], ident32[:])
            grouped = passing("token_grouped", [P, 2 * D], BF16, 2)
            nc.scalar.copy(out=grouped[:].bitcast(F32).rearrange("p (i n u) -> p i n u", i=2, u=2), in_=turned.rearrange("p i u n -> p i n u"))
            live["grouped", which, j] = grouped

        def quantise_tokens(which, j):
            quantise(("grouped", which, j), 2 * D, (which, j), PAIRS)

        def group_vs(g, engine):
            grouped = passing("grouped", [P, K], BF16, 4)
            dst = grouped[:].rearrange("p (a i j) -> p a j i", i=4, j=PACK)
            src = vs_raw[g][:].rearrange("p j (a i) -> p a j i", i=4)
            if engine == "vector":
                nc.vector.tensor_copy(out=dst, in_=src)
            elif engine == "scalar":
                nc.scalar.copy(out=dst, in_=src)
            else:
                nc.gpsimd.tensor_scalar(out=grouped[:].rearrange("p (k j) -> p k j", j=PACK), in0=vs_raw[g][:].rearrange("p j k -> p k j"), scalar1=1.0, scalar2=0.0, op0=ALU.mult, op1=ALU.add)
            live["vs_grouped", g] = grouped

        def quantise_vs(g):
            quantise(("vs_grouped", g), PACK * BANK, ("vs", g), GROUPS)

        def turn_vs(g, h):
            if h == 0:
                live["vsT_grouped", g] = passing("grouped", [P, K], BF16, 4)
            bank = new_bank("scalar")
            turned = bank[:].rearrange("p (j u m) -> p j u m", j=2, u=2)
            for j in range(2):
                words = vs_raw[g][:, 2 * h + j, :].bitcast(F32)
                for u in range(2):
                    nc.tensor.transpose(turned[:, j, u, :], words[:, u::2], ident32[:])
            dst = live["vsT_grouped", g][:].bitcast(F32)[:, h * BANK : (h + 1) * BANK]
            nc.scalar.copy(out=dst.rearrange("p (j m u) -> p j m u", j=2, u=2), in_=turned.rearrange("p j u m -> p j m u"))

        def quantise_vsT(g):
            quantise(("vsT_grouped", g), PACK * D, ("vsT", g), GROUPS)

        def teacher_logits(i, g):
            if g == 0:
                live["teacher", i] = passing("teacher", [P, K], F32, 6)
            codes, plane = live["ht", i // 2]
            cols = slice((i % 2) * P, (i % 2 + 1) * P)
            bank = new_bank("vector")
            nc.tensor.matmul_mx(
                out=bank[:],
                lhsT=codes[:, cols].bitcast(FP8X4),
                lhsT_scale=plane[:, cols],
                rhs=vt_codes[:, 2 * BANK * g : 2 * BANK * (g + 1)].bitcast(FP4X4),
                rhs_scale=vt_plane[:, BANK * g : BANK * (g + 1)],
                start=True,
                stop=True,
            )
            nc.vector.tensor_tensor(
                out=live["teacher", i][:, g * BANK : (g + 1) * BANK].rearrange("n (t m) -> n t m", t=PACK),
                in0=ctr_all[:, g, :].rearrange("n (t m) -> n t m", t=PACK),
                in1=bank[:].rearrange("n (m t) -> n t m", t=PACK),
                op=ALU.subtract,
            )

        def teacher_fold(i):
            folded = passing("folded", [P, K // 2], BF16, 2)
            logits = live["teacher", i]
            nc.vector.tensor_tensor(out=folded[:], in0=logits[:, 0 : K // 2], in1=logits[:, K // 2 : K], op=ALU.min)
            live["folded", i] = folded

        def teacher_min(i):
            least = passing("teacher_least", [P, 1], F32, 4)
            folded = live["folded", i]
            nc.vector.tensor_scalar(out=folded[:], in0=folded[:], scalar1=1.0 / TEACHER_TEMP, scalar2=None, op0=ALU.mult, op1=ALU.min, accum_out=least[:])
            live["teacher_bias", i] = least[:]

        def softmax_exp(who, i):
            logits = live[who, i]
            total = passing("total", [P, 1], F32, 6)
            scale = -1.0 / TEACHER_TEMP if who == "teacher" else -1.0
            nc.scalar.activation(out=logits[:], in_=logits[:], func=ACT.Exp, scale=scale, bias=live[who + "_bias", i], accum_out=total[:])
            live[who + "_total", i] = total

        def student_logits(j, b):
            if b == 0:
                live["studentT", j] = passing("studentT", [P, K // P, 2 * P], F32, 2)
            codes, plane = live["hs", j]
            bank = new_bank("scalar")
            for h in range(2):
                kt = 2 * b + h
                vs_codes, vs_plane = live["vs", kt // 4]
                cols = slice((kt % 4) * P, (kt % 4 + 1) * P)
                nc.tensor.matmul_mx(
                    out=bank[:, h * 2 * P : (h + 1) * 2 * P],
                    lhsT=vs_codes[:, cols].bitcast(FP8X4),
                    lhsT_scale=vs_plane[:, cols],
                    rhs=codes[:].bitcast(FP8X4),
                    rhs_scale=plane[:],
                    start=True,
                    stop=True,
                )
            for h in range(2):
                kt = 2 * b + h
                nc.scalar.activation(out=live["studentT", j][:, kt, :], in_=bank[:, h * 2 * P : (h + 1) * 2 * P], func=ACT.Copy, scale=gs_logit[:, kt : kt + 1])

        def student_turn(i, g):
            if g == 0:
                live["student", i] = passing("student", [P, K], F32, 3)
                live["student_least", i] = passing("student_least", [P, GROUPS], F32, 3)
                live["student_bias", i] = live["student_least", i][:, GROUPS - 1 : GROUPS]
            least = live["student_least", i]
            bank = new_bank("vector")
            for q in range(4):
                nc.tensor.transpose(bank[:, q * P : (q + 1) * P], live["studentT", i // 2][:, 4 * g + q, (i % 2) * P : (i % 2 + 1) * P], ident32[:])
            nc.vector.tensor_scalar(
                out=live["student", i][:, g * BANK : (g + 1) * BANK].rearrange("n (t m) -> n t m", t=PACK),
                in0=bank[:].rearrange("n (m t) -> n t m", t=PACK),
                scalar1=1.0,
                scalar2=least[:, g - 1 : g] if g else None,
                op0=ALU.mult,
                op1=ALU.min,
                accum_out=least[:, g : g + 1],
            )

        def invert_total(who, i):
            inverse = passing("inverse", [P, 1], F32, 6)
            nc.vector.reciprocal(out=inverse[:], in_=live[who + "_total", i][:])
            live[who + "_inverse", i] = inverse

        def normalise(who, i, h, parts, engine):
            e = live[who, i][:, h * K // parts : (h + 1) * K // parts]
            sign = -1.0 if who == "teacher" else 1.0
            eng = nc.vector if engine == "vector" else nc.gpsimd
            eng.tensor_scalar(out=e, in0=e, scalar1=live[who + "_inverse", i][:], scalar2=sign, op0=ALU.mult, op1=ALU.mult)

        def grad_turn(i, g):
            if g == 0:
                live["grad_grouped", i] = passing("grouped", [P, K], BF16, 4)
            bank = new_bank("vector")
            for t in range(PACK):
                cols = slice(g * BANK + t * P, g * BANK + (t + 1) * P)
                dst = bank[:, t * P : (t + 1) * P]
                nc.tensor.matmul(dst, lhsT=live["student", i][:, cols], rhs=ident32[:], start=True, stop=False, is_transpose=True)
                nc.tensor.matmul(dst, lhsT=live["teacher", i][:, cols], rhs=ident32[:], start=False, stop=True, is_transpose=True)
            nc.vector.tensor_tensor(
                out=live["grad_grouped", i][:, g * BANK : (g + 1) * BANK].rearrange("p (n t) -> p n t", t=PACK),
                in0=gs_grad[:, g, :].unsqueeze(1).to_broadcast([P, P, PACK]),
                in1=bank[:].rearrange("p (t n) -> p n t", t=PACK),
                op=ALU.mult,
            )

        def quantise_grad(i, g, n):
            if g == 0:
                live["grad", i] = (passing("grad_codes", [P, K // PACK], U32, 2), passing("grad_plane", [P, K // PACK], U8, 2))
            codes, plane = live["grad", i]
            cols = slice(g * P, (g + n) * P)
            nc.vector.quantize_mx(out=codes[:, cols].bitcast(FP8X4), scales=plane[:, cols], in_=live["grad_grouped", i][:, g * BANK : (g + n) * BANK])

        def feature_pass(dst, i, j, g):
            codes, plane = live["grad", i]
            w_codes, w_plane = live["vsT", g]
            nc.tensor.matmul_mx(
                out=dst,
                lhsT=w_codes[:, j * P : (j + 1) * P].bitcast(FP8X4),
                lhsT_scale=w_plane[:, j * P : (j + 1) * P],
                rhs=codes[:, g * P : (g + 1) * P].bitcast(FP8X4),
                rhs_scale=plane[:, g * P : (g + 1) * P],
                start=(g == 0),
                stop=(g == GROUPS - 1),
            )

        def feature_grad(i):
            bank = new_bank("scalar")
            for j in range(PACK):
                for g in range(GROUPS):
                    feature_pass(bank[:, j * P : (j + 1) * P], i, j, g)
            result = passing("resultT", [P, PACK, P], F32, 2)
            for j in range(PACK):
                nc.scalar.activation(out=result[:, j, :], in_=bank[:, j * P : (j + 1) * P], func=ACT.Copy, scale=c_out[:, j : j + 1])
            live["resultT", i] = result

        def last_feature_passes(g):
            i = TILES - 1
            if g == 0:
                live["last_banks"] = [new_bank("scalar" if j % 2 else "vector") for j in range(PACK)]
            for j in range(PACK):
                feature_pass(live["last_banks"][j][:, 0:P], i, j, g)

        def last_feature_grad():
            result = passing("resultT", [P, PACK, P], F32, 2)
            for j in range(PACK):
                src = live["last_banks"][j][:, 0:P]
                if j % 2:
                    nc.scalar.activation(out=result[:, j, :], in_=src, func=ACT.Copy, scale=c_out[:, j : j + 1])
                else:
                    nc.vector.tensor_scalar(out=result[:, j, :], in0=src, scalar1=c_out[:, j : j + 1], scalar2=None, op0=ALU.mult)
            live["resultT", TILES - 1] = result

        def group_result(i, engine):
            grouped = passing("result_grouped", [P, PACK * P], BF16, 2)
            dst = grouped[:].rearrange("p (n j) -> p n j", j=PACK)
            src = live["resultT", i][:].rearrange("p j n -> p n j")
            if engine == "vector":
                nc.vector.tensor_copy(out=dst, in_=src)
            elif engine == "scalar":
                nc.scalar.copy(out=dst, in_=src)
            else:
                nc.gpsimd.tensor_scalar(out=dst, in0=src, scalar1=1.0, scalar2=0.0, op0=ALU.mult, op1=ALU.add)
            live["result_grouped", i] = grouped

        def store_codes(i):
            cols = slice(i * P, (i + 1) * P)
            nc.vector.quantize_mx(out=out_codes[:, cols].bitcast(FP8X4), scales=out_plane[:, cols], in_=live["result_grouped", i][:])
            nc.sync.dma_start(out=out_1[0].rearrange("p m t -> p (m t)").bitcast(I32)[:, cols], in_=out_codes[:, cols].bitcast(I32))

        def store_scales(lo, hi):
            for q in range(4):
                (nc.scalar if q % 2 and hi == TILES else nc.sync).dma_start(out=out_2[0, 4 * q : 4 * q + 4, lo * P : hi * P].bitcast(I32), in_=out_plane[32 * q : 32 * q + 4, lo * P : hi * P].bitcast(I32))

        def store_result(i):
            bank = new_bank("scalar")
            for j in range(PACK):
                nc.tensor.transpose(bank[:, j * P : (j + 1) * P], live["resultT", i][:, j, :], ident32[:])
            result = passing("result", [P, D], F32, 2)
            nc.scalar.copy(out=result[:].rearrange("n (m j) -> n m j", j=PACK), in_=bank[:].rearrange("n (j m) -> n m j", j=PACK))
            nc.sync.dma_start(out=out_0[i * P : (i + 1) * P, :], in_=result[:])

        steps = dict(load_tokens=load_tokens, load_vs=load_vs, load_vt=load_vt, load_vt_scales=load_vt_scales, load_ctr_rows=load_ctr_rows, load_c_row=load_c_row, load_gs_rows=load_gs_rows, load_columns=load_columns, clear=clear, warm_exp=warm_exp, spread_row=spread_row, gs_columns=gs_columns, scale_columns=scale_columns, scale_hs=scale_hs, turn_tokens=turn_tokens, quantise_tokens=quantise_tokens, group_vs=group_vs, quantise_vs=quantise_vs, turn_vs=turn_vs, quantise_vsT=quantise_vsT, teacher_logits=teacher_logits, teacher_fold=teacher_fold, teacher_min=teacher_min, softmax_exp=softmax_exp, student_logits=student_logits, student_turn=student_turn, invert_total=invert_total, normalise=normalise, grad_turn=grad_turn, quantise_grad=quantise_grad, feature_grad=feature_grad, last_feature_passes=last_feature_passes, last_feature_grad=last_feature_grad, group_result=group_result, store_codes=store_codes, store_scales=store_scales, store_result=store_result)
        plan = [(steps[name], args) for name, args in make_plan(PARAMS)]

        with tc.manual_schedule():
            for step, args in plan:
                step(*args)
